import numpy as np
import ml_dtypes


def mxq(x, axis, fmt="e4m3"):
    dtype, down = {"e4m3": (ml_dtypes.float8_e4m3fn, 7), "e5m2": (ml_dtypes.float8_e5m2, 14)}[fmt]
    v = np.moveaxis(np.asarray(x, np.float32).astype(ml_dtypes.bfloat16).astype(np.float64), axis, -1)
    blocks = v.reshape(v.shape[:-1] + (-1, 32))
    amax = np.abs(blocks).max(-1, keepdims=True)
    byte = np.maximum(np.where(amax > 0, np.frexp(amax)[1] - 1 + 127, 0) - down, 1)
    scale = np.exp2(byte - 127.0)
    codes = (blocks / scale).astype(np.float32).astype(dtype).astype(np.float64)
    return np.moveaxis((codes * scale).reshape(v.shape), -1, axis)


WIDE = False


def mx_kscale(k):
    if not WIDE:
        return np.ones(k)
    levels = np.array([10, -10, 5, -5, 0])
    if k % 512:
        return np.exp2(np.random.permutation(np.resize(levels, k // 32))).repeat(32)
    a = np.empty((k // 512, 16))
    for p in range(k // 512):
        a[p, :8] = np.random.permutation(np.resize(levels, 8))
        for g in range(8):
            far = levels[np.abs(levels - a[p, g]) >= 10]
            a[p, g + 8] = far[np.random.randint(len(far))]
    return np.exp2(a.ravel()).repeat(32)


def f64(x):
    return np.asarray(x).astype(np.float64)


def striped(idx):
    return np.tile(np.asarray(idx).reshape(-1, 16).T, (8, 1)).astype(np.uint16)


def unstriped(offs):
    return offs[:16].T.reshape(-1).astype(np.int64)


E2M1 = np.array([0.0, 0.5, 1.0, 1.5, 2.0, 3.0, 4.0, 6.0, -0.0, -0.5, -1.0, -1.5, -2.0, -3.0, -4.0, -6.0])


def pack_weight(w, fmt):
    k, n = w.shape
    w = f64(np.asarray(w, np.float32).astype(ml_dtypes.bfloat16)).reshape(k // 32, 32, n)
    amax = np.abs(w).max(1)
    if fmt == "e4m3":
        byte = np.frexp(amax)[1] - 1 + 127 - 7
    else:
        mant, ex = np.frexp(amax / 6.0)
        byte = np.where(mant > 0.5, ex, ex - 1) + 127
    byte = np.clip(np.where(amax > 0, byte, 1), 1, 254)
    scaled = (w * np.exp2(127.0 - byte)[:, None, :]).reshape(k, n).astype(np.float32)
    by_word = np.ascontiguousarray(scaled.reshape(k // 512, 128, 4, n).transpose(0, 1, 3, 2))
    if fmt == "e4m3":
        words = by_word.astype(ml_dtypes.float8_e4m3fn).view(np.uint8)
    else:
        c = by_word.astype(ml_dtypes.float4_e2m1fn).view(np.uint8) & 0xF
        words = (c[..., 0::2] | (c[..., 1::2] << 4)).reshape(k // 512, 128, 2 * n)
    return np.ascontiguousarray(words), np.ascontiguousarray(byte.astype(np.uint8).reshape(k // 512, 16, n))


def unpack_weight(words, scales, fmt):
    g, _, n = scales.shape
    words = np.ascontiguousarray(words).reshape(g, 128, n, -1)
    if fmt == "e4m3":
        vals = words.view(ml_dtypes.float8_e4m3fn).astype(np.float64)
    else:
        nib = np.empty((g, 128, n, 4), np.uint8)
        nib[..., 0::2] = words & 0xF
        nib[..., 1::2] = words >> 4
        vals = E2M1[nib]
    vals = vals * np.repeat(np.exp2(scales.astype(np.float64) - 127.0), 8, axis=1)[..., None]
    return vals.transpose(0, 1, 3, 2).reshape(g * 512, n)


def sigmoid(v):
    return 1.0 / (1.0 + np.exp(-v))


D, T, I, Q, E, H = 512, 2048, 512, 128, 512, 32


def setup_inputs():
    n = np.random.standard_normal
    idx = np.random.permutation(T)[:I]
    fd = mx_kscale(D)
    fi = mx_kscale(I)
    keysp = pack_weight(n((D, T)) / fd[:, None], "e4m3")
    return {
        "query": (n((D, Q)) * 1.2 / np.sqrt(D) * fd[:, None]).astype(np.float32),
        "keys_words": keysp[0],
        "keys_scales": keysp[1],
        "guess": np.tile(np.random.uniform(0.05, 0.3, T), (128, 1)).astype(np.float32),
        "steep": np.tile(np.random.uniform(1.0, 3.0, T), (128, 1)).astype(np.float32),
        "thr": np.tile(np.random.uniform(-0.5, 1.0, T), (128, 1)).astype(np.float32),
        "lam": (np.random.uniform(0.6, 1.5, (Q, 1))).astype(np.float32),
        "eager": (np.random.uniform(0.8, 2.0, (Q, 1))).astype(np.float32),
        "thresh": (np.random.uniform(1.5, 4.0, (Q, 1))).astype(np.float32),
        "os": (np.random.uniform(4.0, 16.0, (1, I)) * fi).astype(np.float32),
        "vals": (n((E, T))).astype(np.float32),
        "vsc": (np.random.uniform(0.5, 2.0, (1, I)) / fi).astype(np.float32),
        "offs": striped(idx),
    }


def reference(query, keys_words, keys_scales, guess, steep, thr, lam, eager, thresh, os, vals, vsc, offs):
    idx = unstriped(offs)
    keysu = unpack_weight(keys_words, keys_scales, "e4m3")
    queryq = mxq(f64(query), 0, "e4m3")
    keysidxg = keysu[:, idx]
    a = queryq.T @ keysidxg
    sg = sigmoid((a - f64(thr)[:1][:, idx]) * f64(steep)[:1][:, idx])
    s = np.log(sg * (1.0 - f64(guess)[:1][:, idx]) + f64(guess)[:1][:, idx]) * f64(lam)
    m0 = np.max(s, axis=1, keepdims=True)
    m1 = np.mean(s, axis=1, keepdims=True)
    p = np.exp(s - m0)
    gt0 = sigmoid((m0 - m1) * f64(eager) - f64(thresh))
    w = p / np.sum(p, axis=1, keepdims=True) * gt0
    wo1 = w * f64(os)
    wt1 = wo1.T
    vg = f64(vals)[:, idx].reshape(E, H, I // H).mean(axis=2)
    vgr = np.repeat(vg, I // H, axis=1)
    vd = (f64(vals)[:, idx] - vgr) * f64(vsc)
    vt1 = vd.T
    wt1q = mxq(wt1, 0, "e4m3")
    vt1q = mxq(vt1, 0, "e4m3")
    o = wt1q.T @ vt1q
    return o

@@ -1,0 +1,227 @@
+from contextlib import ExitStack
+
+import concourse.mybir as mybir
+from concourse.masks import make_identity
+
+D, T, I, Q, E, H = 512, 2048, 512, 128, 512, 32
+FLOPS = 2 * Q * I * D + 2 * Q * I * E
+BYTES = 4 * D * Q + D * T + 16 * T + 3 * 4 * T + 3 * 4 * Q + 2 * 4 * I + 4 * E * T + 2 * I + 4 * Q * E
+
+F32 = mybir.dt.float32
+BF16 = mybir.dt.bfloat16
+I32 = mybir.dt.int32
+U32 = mybir.dt.uint32
+U16 = mybir.dt.uint16
+U8 = mybir.dt.uint8
+FP8X4 = mybir.dt.float8_e4m3fn_x4
+ALU = mybir.AluOpType
+ACT = mybir.ActivationFunctionType
+AXIS_X = mybir.AxisListType.X
+
+P = 128
+PACK = 4
+STRETCH = I // H
+BLOCKS = E // P
+ROW = P - 1
+
+
+def tile_attend_answerodds_abstaining_centredvalues_kernel(
+    tc, query, keys_words, keys_scales, guess, steep, thr, lam, eager, thresh, slot_factor, vals, vsc, offs, out
+):
+    nc = tc.nc
+    with ExitStack() as ctx:
+        keep = ctx.enter_context(tc.tile_pool(name="keep", bufs=1))
+        psum = ctx.enter_context(tc.psum_pool(name="psum", bufs=1))
+
+        offsets = keep.tile([P, I // 16], U16, name="offsets")
+        key_words = keep.tile([P, T], U32, name="key_words")
+        key_bytes = keep.tile([P, T], U8, name="key_bytes")
+        thr_pool = keep.tile([P, T], F32, name="thr_pool")
+        steep_pool = keep.tile([P, T], F32, name="steep_pool")
+        guess_pool = keep.tile([P, T], F32, name="guess_pool")
+        query_raw = keep.tile([P, PACK, Q], F32, name="query_raw")
+        val_pool = [keep.tile([P, T], F32, name=f"val_pool{b}") for b in range(BLOCKS)]
+
+        nc.vector.memset(key_bytes[:].bitcast(I32), 0)
+        nc.vector.memset(thr_pool[0:ROW, :], 0.0)
+        nc.vector.memset(steep_pool[0:ROW, :], 0.0)
+        nc.vector.memset(guess_pool[0:ROW, :], 0.0)
+
+        nc.scalar.dma_start(key_words[:].bitcast(I32), keys_words[0].rearrange("p n t -> p (n t)").bitcast(I32))
+        nc.sync.dma_start(offsets[:], offs)
+        nc.sync.dma_start(thr_pool[ROW:P, :], thr[0:1, :])
+        nc.sync.dma_start(steep_pool[ROW:P, :], steep[0:1, :])
+        for g in range(4):
+            nc.sync.dma_start(key_bytes[32 * g : 32 * g + 4, :].bitcast(I32), keys_scales[0, 4 * g : 4 * g + 4, :].bitcast(I32))
+        nc.sync.dma_start(query_raw[:], query.rearrange("(p t) q -> p t q", t=PACK))
+        nc.sync.dma_start(guess_pool[ROW:P, :], guess[0:1, :])
+        for b in range(2):
+            nc.sync.dma_start(val_pool[b][:], vals[b * P : (b + 1) * P, :])
+        vsc_col = keep.tile([P, PACK], F32, name="vsc_col")
+        nc.sync.dma_start(vsc_col[:], vsc.rearrange("o (p t) -> (o p) t", t=PACK))
+        lam_col = keep.tile([P, 1], F32, name="lam_col")
+        nc.sync.dma_start(lam_col[:], lam)
+        eager_col = keep.tile([P, 1], F32, name="eager_col")
+        nc.sync.dma_start(eager_col[:], eager)
+        thresh_col = keep.tile([P, 1], F32, name="thresh_col")
+        nc.sync.dma_start(thresh_col[:], thresh)
+        factor_col = keep.tile([P, PACK], F32, name="factor_col")
+        nc.sync.dma_start(factor_col[:], slot_factor.rearrange("o (p t) -> (o p) t", t=PACK))
+        for b in range(2, BLOCKS):
+            nc.sync.dma_start(val_pool[b][:], vals[b * P : (b + 1) * P, :])
+
+        ident = keep.tile([P, P], F32, name="ident")
+        make_identity(nc, ident[:])
+
+        def turn_row(row_tile, bank):
+            for j in range(PACK):
+                nc.tensor.transpose(bank[:, j, :], row_tile[:, j * P : (j + 1) * P], ident[:])
+
+        thr_row = keep.tile([P, I], F32, name="thr_row")
+        nc.scalar.activation(thr_row[:], thr_pool[:].indirect(offsets[:]), ACT.Copy)
+        steep_row = keep.tile([P, I], F32, name="steep_row")
+        nc.scalar.activation(steep_row[:], steep_pool[:].indirect(offsets[:]), ACT.Copy)
+        guess_row = keep.tile([P, I], F32, name="guess_row")
+        nc.scalar.activation(guess_row[:], guess_pool[:].indirect(offsets[:]), ACT.Copy)
+        query_bf = keep.tile([P, Q, PACK], BF16, name="query_bf", align_bytes=64)
+        nc.scalar.copy(query_bf[:], query_raw[:].rearrange("p t q -> p q t"))
+
+        picked_words = keep.tile([P, I], U32, name="picked_words", align_bytes=64)
+        nc.vector.tensor_copy(picked_words[:], key_words[:].indirect(offsets[:]))
+        picked_bytes = keep.tile([P, I], U8, name="picked_bytes", align_bytes=64)
+        nc.vector.tensor_copy(picked_bytes[:], key_bytes[:].indirect(offsets[:]))
+        query_codes = keep.tile([P, Q], U32, name="query_codes", align_bytes=64)
+        query_scales = keep.tile([P, Q], U8, name="query_scales", align_bytes=64)
+        nc.vector.quantize_mx(query_codes[:].bitcast(FP8X4), query_scales[:], query_bf[:].rearrange("p q t -> p (q t)"))
+
+        thr_bank = psum.tile([P, PACK, P], F32, name="thr_bank", tag="bank_a")
+        turn_row(thr_row, thr_bank)
+        steep_bank = psum.tile([P, PACK, P], F32, name="steep_bank", tag="bank_b")
+        turn_row(steep_row, steep_bank)
+        steep_col = keep.tile([P, PACK], F32, name="steep_col")
+        nc.vector.tensor_copy(steep_col[:], steep_bank[:, :, ROW])
+        shift_col = keep.tile([P, PACK], F32, name="shift_col")
+        nc.vector.scalar_tensor_tensor(shift_col[:], thr_bank[:, :, ROW], -1.0, steep_col[:], ALU.mult, ALU.mult)
+
+        score_bank = psum.tile([P, PACK, Q], F32, name="score_bank")
+        for j in range(PACK):
+            cols = slice(j * P, (j + 1) * P)
+            nc.tensor.matmul_mx(
+                score_bank[:, j, :], lhsT=picked_words[:, cols].bitcast(FP8X4), lhsT_scale=picked_bytes[:, cols],
+                rhs=query_codes[:].bitcast(FP8X4), rhs_scale=query_scales[:], start=True, stop=True,
+            )
+        sig = keep.tile([P, PACK, Q], F32, name="sig")
+        for j in range(PACK):
+            nc.scalar.activation(sig[:, j, :], score_bank[:, j, :], ACT.Sigmoid, bias=shift_col[:, j : j + 1], scale=steep_col[:, j : j + 1])
+
+        guess_bank = psum.tile([P, PACK, P], F32, name="guess_bank", tag="bank_c")
+        turn_row(guess_row, guess_bank)
+        guess_col = keep.tile([P, PACK], F32, name="guess_col")
+        nc.vector.tensor_copy(guess_col[:], guess_bank[:, :, ROW])
+        rest_col = keep.tile([P, PACK], F32, name="rest_col")
+        nc.vector.tensor_scalar(rest_col[:], guess_bank[:, :, ROW], -1.0, 1.0, ALU.mult, ALU.add)
+        neg_lam = keep.tile([P, 1], F32, name="neg_lam")
+        nc.vector.tensor_scalar(neg_lam[:], lam_col[:], -1.0, None, ALU.mult)
+
+        log_chance = keep.tile([P, PACK, Q], F32, name="log_chance")
+        for j in range(PACK):
+            nc.scalar.activation(log_chance[:, j, :], sig[:, j, :], ACT.Ln, bias=guess_col[:, j : j + 1], scale=rest_col[:, j : j + 1])
+        log_bank = psum.tile([P, PACK, P], F32, name="log_bank")
+        for j in range(PACK):
+            nc.tensor.transpose(log_bank[:, j, :], log_chance[:, j, :], ident[:])
+
+        picked_vals = [keep.tile([P, I], F32, name=f"picked_vals{b}") for b in range(BLOCKS)]
+        val_codes = [keep.tile([P, P], U32, name=f"val_codes{b}", align_bytes=64) for b in range(BLOCKS)]
+        val_scales = [keep.tile([P, P], U8, name=f"val_scales{b}", align_bytes=64) for b in range(BLOCKS)]
+        val_banks = {}
+
+        def gather_vals(b, on_vector):
+            window = val_pool[b][:].indirect(offsets[:])
+            if on_vector:
+                nc.vector.tensor_copy(picked_vals[b][:], window)
+            else:
+                nc.scalar.activation(picked_vals[b][:], window, ACT.Copy)
+
+        def centre_vals(b):
+            sums = keep.tile([P, H], F32, name=f"sums{b}")
+            nc.vector.tensor_reduce(sums[:], picked_vals[b][:].rearrange("p (h s) -> p h s", s=STRETCH), AXIS_X, ALU.add)
+            neg_mean = keep.tile([P, H, PACK], F32, name=f"neg_mean{b}")
+            nc.vector.tensor_scalar(
+                neg_mean[:], sums[:].rearrange("p (h o) -> p h o", o=1).to_broadcast([P, H, PACK]), -1.0 / STRETCH, None, ALU.mult
+            )
+            bank = psum.tile([P, PACK, P], F32, name=f"val_bank{b}", tag="val_bank", bufs=3)
+            for t in range(PACK):
+                nc.tensor.matmul(bank[:, t, :], picked_vals[b][:, t : I : PACK], ident[:], start=(t == 0), stop=False, is_transpose=True)
+            for t in range(PACK):
+                nc.tensor.matmul(
+                    bank[:, t, :], neg_mean[:].rearrange("p h r -> p (h r)"), ident[:], start=False, stop=(t == PACK - 1), is_transpose=True
+                )
+            val_banks[b] = bank
+
+        def scale_and_quantise(bank, col, codes, scales, name):
+            staged = keep.tile([P, P, PACK], BF16, name=name, align_bytes=64)
+            nc.vector.tensor_tensor(
+                staged[:], bank[:].rearrange("p t x -> p x t"),
+                col[:].rearrange("p (o t) -> p o t", o=1).to_broadcast([P, P, PACK]), ALU.mult,
+            )
+            nc.vector.quantize_mx(codes[:].bitcast(FP8X4), scales[:], staged[:].rearrange("p x t -> p (x t)"))
+
+        gather_vals(0, True)
+        centre_vals(0)
+        gather_vals(1, True)
+        centre_vals(1)
+
+        neg_s = keep.tile([P, I], F32, name="neg_s")
+        neg_max = keep.tile([P, 1], F32, name="neg_max")
+        nc.vector.tensor_scalar(neg_s[:], log_bank[:].rearrange("p j s -> p (j s)"), neg_lam[:], None, ALU.mult, ALU.min, accum_out=neg_max[:])
+        neg_sum = keep.tile([P, 1], F32, name="neg_sum")
+        nc.vector.tensor_reduce(neg_sum[:], neg_s[:], AXIS_X, ALU.add)
+        mean_less_max = keep.tile([P, 1], F32, name="mean_less_max")
+        nc.vector.tensor_scalar(mean_less_max[:], neg_sum[:], -1.0 / I, neg_max[:], ALU.mult, ALU.add)
+        probs = keep.tile([P, I], F32, name="probs")
+        prob_sum = keep.tile([P, 1], F32, name="prob_sum")
+        nc.scalar.activation(probs[:], neg_s[:], ACT.Exp, bias=neg_max[:], scale=-1.0, accum_out=prob_sum[:])
+        odds = keep.tile([P, 1], F32, name="odds")
+        nc.scalar.activation(odds[:], mean_less_max[:], ACT.Exp, bias=thresh_col[:], scale=eager_col[:])
+
+        scale_and_quantise(val_banks[0], vsc_col, val_codes[0], val_scales[0], "val_bf0")
+        gather_vals(2, False)
+        scale_and_quantise(val_banks[1], vsc_col, val_codes[1], val_scales[1], "val_bf1")
+
+        denom = keep.tile([P, 1], F32, name="denom")
+        nc.vector.tensor_scalar(denom[:], odds[:], 1.0, prob_sum[:], ALU.add, ALU.mult)
+        gain = keep.tile([P, 1], F32, name="gain")
+        nc.vector.reciprocal(gain[:], denom[:])
+        weights = keep.tile([P, PACK, P], F32, name="weights")
+        nc.vector.tensor_scalar(weights[:], probs[:].rearrange("q (p t) -> q t p", t=PACK), gain[:], None, ALU.mult)
+        weight_bank = psum.tile([P, PACK, Q], F32, name="weight_bank", tag="bank_a")
+        for t in range(PACK):
+            nc.tensor.transpose(weight_bank[:, t, :], weights[:, t, :], ident[:])
+        centre_vals(2)
+        gather_vals(3, False)
+        weight_codes = keep.tile([P, Q], U32, name="weight_codes", align_bytes=64)
+        weight_scales = keep.tile([P, Q], U8, name="weight_scales", align_bytes=64)
+        scale_and_quantise(weight_bank, factor_col, weight_codes, weight_scales, "weight_bf")
+        centre_vals(3)
+        scale_and_quantise(val_banks[2], vsc_col, val_codes[2], val_scales[2], "val_bf2")
+
+        def product(bank_cols, b):
+            nc.tensor.matmul_mx(
+                bank_cols, lhsT=weight_codes[:].bitcast(FP8X4), lhsT_scale=weight_scales[:],
+                rhs=val_codes[b][:].bitcast(FP8X4), rhs_scale=val_scales[b][:], start=True, stop=True,
+            )
+
+        last = BLOCKS - 1
+        early_bank = psum.tile([P, last, P], F32, name="early_bank", tag="bank_b")
+        for b in range(last):
+            product(early_bank[:, b, :], b)
+        early_out = keep.tile([P, last * P], F32, name="early_out")
+        nc.scalar.copy(early_out[:], early_bank[:].rearrange("p b x -> p (b x)"))
+        nc.sync.dma_start(out[:, 0 : last * P], early_out[:])
+
+        scale_and_quantise(val_banks[last], vsc_col, val_codes[last], val_scales[last], "val_bf3")
+        last_bank = psum.tile([P, P], F32, name="last_bank", tag="bank_c")
+        product(last_bank[:], last)
+        last_out = keep.tile([P, P], F32, name="last_out")
+        nc.scalar.copy(last_out[:], last_bank[:])
+        nc.sync.dma_start(out[:, last * P : E], last_out[:])

@@ -35,43 +35,46 @@ def tile_attend_answerodds_abstaining_centredvalues_kernel(
 
         offsets = keep.tile([P, I // 16], U16, name="offsets")
         key_words = keep.tile([P, T], U32, name="key_words")
-        key_bytes = keep.tile([P, T], U8, name="key_bytes")
+        key_bytes = keep.tile([P, T], U8, name="key_bytes", tag="slot_k", align_bytes=64)
         thr_pool = keep.tile([P, T], F32, name="thr_pool")
         steep_pool = keep.tile([P, T], F32, name="steep_pool")
-        guess_pool = keep.tile([P, T], F32, name="guess_pool")
-        query_raw = keep.tile([P, PACK, Q], F32, name="query_raw")
-        val_pool = [keep.tile([P, T], F32, name=f"val_pool{b}") for b in range(BLOCKS)]
+        guess_pool = keep.tile([P, T], F32, name="guess_pool", align_bytes=64)
+        query_raw = keep.tile([P, PACK, Q], F32, name="query_raw", align_bytes=64)
+        val_pool = [keep.tile([P, T], F32, name=f"val_pool{b}", align_bytes=64) for b in range(BLOCKS)]
 
         nc.vector.memset(key_bytes[:].bitcast(I32), 0)
         nc.vector.memset(thr_pool[0:ROW, :], 0.0)
         nc.vector.memset(steep_pool[0:ROW, :], 0.0)
         nc.vector.memset(guess_pool[0:ROW, :], 0.0)
 
-        nc.scalar.dma_start(key_words[:].bitcast(I32), keys_words[0].rearrange("p n t -> p (n t)").bitcast(I32))
+        zero_col = keep.tile([P, 1], F32, name="zero_col")
+        nc.gpsimd.memset(zero_col[:], 0.0)
+        ident = keep.tile([P, P], F32, name="ident")
+        make_identity(nc, ident[:])
+
         nc.sync.dma_start(offsets[:], offs)
+        nc.scalar.dma_start(steep_pool[ROW:P, :], steep[0:1, :])
+        nc.scalar.dma_start(key_words[:].bitcast(I32), keys_words[0].rearrange("p n t -> p (n t)").bitcast(I32))
+        warm = keep.tile([P, 1], F32, name="warm")
+        nc.scalar.activation(warm[:], zero_col[:], ACT.Sigmoid)
+        nc.scalar.dma_start(guess_pool[ROW:P, :], guess[0:1, :])
         nc.sync.dma_start(thr_pool[ROW:P, :], thr[0:1, :])
-        nc.sync.dma_start(steep_pool[ROW:P, :], steep[0:1, :])
         for g in range(4):
             nc.sync.dma_start(key_bytes[32 * g : 32 * g + 4, :].bitcast(I32), keys_scales[0, 4 * g : 4 * g + 4, :].bitcast(I32))
         nc.sync.dma_start(query_raw[:], query.rearrange("(p t) q -> p t q", t=PACK))
-        nc.sync.dma_start(guess_pool[ROW:P, :], guess[0:1, :])
-        for b in range(2):
-            nc.sync.dma_start(val_pool[b][:], vals[b * P : (b + 1) * P, :])
         vsc_col = keep.tile([P, PACK], F32, name="vsc_col")
-        nc.sync.dma_start(vsc_col[:], vsc.rearrange("o (p t) -> (o p) t", t=PACK))
         lam_col = keep.tile([P, 1], F32, name="lam_col")
-        nc.sync.dma_start(lam_col[:], lam)
         eager_col = keep.tile([P, 1], F32, name="eager_col")
-        nc.sync.dma_start(eager_col[:], eager)
         thresh_col = keep.tile([P, 1], F32, name="thresh_col")
-        nc.sync.dma_start(thresh_col[:], thresh)
         factor_col = keep.tile([P, PACK], F32, name="factor_col")
-        nc.sync.dma_start(factor_col[:], slot_factor.rearrange("o (p t) -> (o p) t", t=PACK))
-        for b in range(2, BLOCKS):
+        loads_after_block = {
+            2: [(eager_col, eager), (thresh_col, thresh)],
+            3: [(factor_col, slot_factor.rearrange("o (p t) -> (o p) t", t=PACK))],
+        }
+        for b in range(BLOCKS):
             nc.sync.dma_start(val_pool[b][:], vals[b * P : (b + 1) * P, :])
-
-        ident = keep.tile([P, P], F32, name="ident")
-        make_identity(nc, ident[:])
+            for column, source in loads_after_block.get(b, []):
+                nc.sync.dma_start(column[:], source)
 
         def turn_row(row_tile, bank):
             for j in range(PACK):
@@ -81,47 +84,56 @@ def tile_attend_answerodds_abstaining_centredvalues_kernel(
         nc.scalar.activation(thr_row[:], thr_pool[:].indirect(offsets[:]), ACT.Copy)
         steep_row = keep.tile([P, I], F32, name="steep_row")
         nc.scalar.activation(steep_row[:], steep_pool[:].indirect(offsets[:]), ACT.Copy)
-        guess_row = keep.tile([P, I], F32, name="guess_row")
-        nc.scalar.activation(guess_row[:], guess_pool[:].indirect(offsets[:]), ACT.Copy)
-        query_bf = keep.tile([P, Q, PACK], BF16, name="query_bf", align_bytes=64)
-        nc.scalar.copy(query_bf[:], query_raw[:].rearrange("p t q -> p q t"))
-
-        picked_words = keep.tile([P, I], U32, name="picked_words", align_bytes=64)
-        nc.vector.tensor_copy(picked_words[:], key_words[:].indirect(offsets[:]))
-        picked_bytes = keep.tile([P, I], U8, name="picked_bytes", align_bytes=64)
-        nc.vector.tensor_copy(picked_bytes[:], key_bytes[:].indirect(offsets[:]))
-        query_codes = keep.tile([P, Q], U32, name="query_codes", align_bytes=64)
-        query_scales = keep.tile([P, Q], U8, name="query_scales", align_bytes=64)
-        nc.vector.quantize_mx(query_codes[:].bitcast(FP8X4), query_scales[:], query_bf[:].rearrange("p q t -> p (q t)"))
-
         thr_bank = psum.tile([P, PACK, P], F32, name="thr_bank", tag="bank_a")
         turn_row(thr_row, thr_bank)
         steep_bank = psum.tile([P, PACK, P], F32, name="steep_bank", tag="bank_b")
         turn_row(steep_row, steep_bank)
+        neg_thr_col = keep.tile([P, PACK], F32, name="neg_thr_col")
+        nc.scalar.activation(neg_thr_col[:], thr_bank[:, :, ROW], ACT.Copy, scale=-1.0)
         steep_col = keep.tile([P, PACK], F32, name="steep_col")
-        nc.vector.tensor_copy(steep_col[:], steep_bank[:, :, ROW])
+        nc.scalar.activation(steep_col[:], steep_bank[:, :, ROW], ACT.Copy)
         shift_col = keep.tile([P, PACK], F32, name="shift_col")
-        nc.vector.scalar_tensor_tensor(shift_col[:], thr_bank[:, :, ROW], -1.0, steep_col[:], ALU.mult, ALU.mult)
+        nc.gpsimd.tensor_tensor(shift_col[:], neg_thr_col[:], steep_col[:], ALU.mult)
+        guess_row = keep.tile([P, I], F32, name="guess_row")
+        nc.scalar.activation(guess_row[:], guess_pool[:].indirect(offsets[:]), ACT.Copy)
+        guess_bank = psum.tile([P, PACK, P], F32, name="guess_bank", tag="bank_c")
+        turn_row(guess_row, guess_bank)
+        guess_col = keep.tile([P, PACK], F32, name="guess_col")
+        nc.scalar.activation(guess_col[:], guess_bank[:, :, ROW], ACT.Copy)
+        rest_col = keep.tile([P, PACK], F32, name="rest_col")
+        nc.gpsimd.tensor_scalar(rest_col[:], guess_col[:], -1.0, 1.0, ALU.mult, ALU.add)
 
-        score_bank = psum.tile([P, PACK, Q], F32, name="score_bank")
+        nc.scalar.dma_start(vsc_col[:], vsc.rearrange("o (p t) -> (o p) t", t=PACK))
+        nc.scalar.dma_start(lam_col[:], lam)
+
+        picked_bytes = keep.tile([P, I], U8, name="picked_bytes", align_bytes=64)
+        nc.vector.tensor_copy(picked_bytes[:], key_bytes[:].indirect(offsets[:]))
+        query_bf = keep.tile([P, Q, PACK], BF16, name="query_bf", align_bytes=64)
+        nc.vector.tensor_copy(query_bf[:], query_raw[:].rearrange("p t q -> p q t"))
+        query_codes = keep.tile([P, Q], U32, name="query_codes", align_bytes=64)
+        query_scales = keep.tile([P, Q], U8, name="query_scales", align_bytes=64)
+        nc.vector.quantize_mx(query_codes[:].bitcast(FP8X4), query_scales[:], query_bf[:].rearrange("p q t -> p (q t)"))
+        picked_words = keep.tile([P, I], U32, name="picked_words", tag="query_raw", align_bytes=64)
+        nc.vector.tensor_copy(picked_words[:], key_words[:].indirect(offsets[:]))
+
+        score_bank = psum.tile([P, PACK, Q], F32, name="score_bank", tag="bank_b")
         for j in range(PACK):
             cols = slice(j * P, (j + 1) * P)
             nc.tensor.matmul_mx(
                 score_bank[:, j, :], lhsT=picked_words[:, cols].bitcast(FP8X4), lhsT_scale=picked_bytes[:, cols],
                 rhs=query_codes[:].bitcast(FP8X4), rhs_scale=query_scales[:], start=True, stop=True,
             )
-        sig = keep.tile([P, PACK, Q], F32, name="sig")
+        sig = keep.tile([P, PACK, Q], F32, name="sig", tag="guess_pool", align_bytes=64)
         for j in range(PACK):
             nc.scalar.activation(sig[:, j, :], score_bank[:, j, :], ACT.Sigmoid, bias=shift_col[:, j : j + 1], scale=steep_col[:, j : j + 1])
 
-        guess_bank = psum.tile([P, PACK, P], F32, name="guess_bank", tag="bank_c")
-        turn_row(guess_row, guess_bank)
-        guess_col = keep.tile([P, PACK], F32, name="guess_col")
-        nc.vector.tensor_copy(guess_col[:], guess_bank[:, :, ROW])
-        rest_col = keep.tile([P, PACK], F32, name="rest_col")
-        nc.vector.tensor_scalar(rest_col[:], guess_bank[:, :, ROW], -1.0, 1.0, ALU.mult, ALU.add)
+        warm_ln = keep.tile([P, 1], F32, name="warm_ln")
+        nc.scalar.activation(warm_ln[:], sig[:, PACK - 1, 0:1], ACT.Ln)
         neg_lam = keep.tile([P, 1], F32, name="neg_lam")
-        nc.vector.tensor_scalar(neg_lam[:], lam_col[:], -1.0, None, ALU.mult)
+        nc.gpsimd.tensor_scalar(neg_lam[:], lam_col[:], -1.0, 0.0, ALU.mult, ALU.add)
+
+        lam_share = keep.tile([P, 1], F32, name="lam_share")
+        nc.gpsimd.tensor_scalar(lam_share[:], lam_col[:], 1.0 / I, 0.0, ALU.mult, ALU.add)
 
         log_chance = keep.tile([P, PACK, Q], F32, name="log_chance")
         for j in range(PACK):
@@ -130,26 +142,36 @@ def tile_attend_answerodds_abstaining_centredvalues_kernel(
         for j in range(PACK):
             nc.tensor.transpose(log_bank[:, j, :], log_chance[:, j, :], ident[:])
 
-        picked_vals = [keep.tile([P, I], F32, name=f"picked_vals{b}") for b in range(BLOCKS)]
+        log_sum_bank = psum.tile([P, P], F32, name="log_sum_bank")
+        for j in range(PACK):
+            nc.tensor.matmul(log_sum_bank[:], log_chance[:, j, :], ident[:], start=(j == 0), stop=(j == PACK - 1), is_transpose=True)
+
+        picked_vals = {}
         val_codes = [keep.tile([P, P], U32, name=f"val_codes{b}", align_bytes=64) for b in range(BLOCKS)]
         val_scales = [keep.tile([P, P], U8, name=f"val_scales{b}", align_bytes=64) for b in range(BLOCKS)]
         val_banks = {}
+        neg_means = {}
 
-        def gather_vals(b, on_vector):
+        def gather_vals(b, on_vector, tag):
+            picked_vals[b] = keep.tile([P, I], F32, name=f"picked_vals{b}", tag=tag, align_bytes=64)
             window = val_pool[b][:].indirect(offsets[:])
             if on_vector:
                 nc.vector.tensor_copy(picked_vals[b][:], window)
             else:
                 nc.scalar.activation(picked_vals[b][:], window, ACT.Copy)
 
-        def centre_vals(b):
-            sums = keep.tile([P, H], F32, name=f"sums{b}")
+        def centre_vals(b, sums_tag, mean_tag):
+            sums = keep.tile([P, H], F32, name=f"sums{b}", tag=sums_tag)
             nc.vector.tensor_reduce(sums[:], picked_vals[b][:].rearrange("p (h s) -> p h s", s=STRETCH), AXIS_X, ALU.add)
-            neg_mean = keep.tile([P, H, PACK], F32, name=f"neg_mean{b}")
+            neg_mean = keep.tile([P, H, PACK], F32, name=f"neg_mean{b}", tag=mean_tag)
             nc.vector.tensor_scalar(
                 neg_mean[:], sums[:].rearrange("p (h o) -> p h o", o=1).to_broadcast([P, H, PACK]), -1.0 / STRETCH, None, ALU.mult
             )
-            bank = psum.tile([P, PACK, P], F32, name=f"val_bank{b}", tag="val_bank", bufs=3)
+            neg_means[b] = neg_mean
+
+        def turn_vals(b, bank_tag):
+            neg_mean = neg_means[b]
+            bank = psum.tile([P, PACK, P], F32, name=f"val_bank{b}", tag=bank_tag)
             for t in range(PACK):
                 nc.tensor.matmul(bank[:, t, :], picked_vals[b][:, t : I : PACK], ident[:], start=(t == 0), stop=False, is_transpose=True)
             for t in range(PACK):
@@ -166,26 +188,30 @@ def tile_attend_answerodds_abstaining_centredvalues_kernel(
             )
             nc.vector.quantize_mx(codes[:].bitcast(FP8X4), scales[:], staged[:].rearrange("p x t -> p (x t)"))
 
-        gather_vals(0, True)
-        centre_vals(0)
-        gather_vals(1, True)
-        centre_vals(1)
+        gather_vals(0, True, "slot_a")
+        centre_vals(0, "sums0", "mean0")
+        turn_vals(0, "bank_b")
+        gather_vals(1, True, "slot_b")
+        centre_vals(1, "sums1", "log_chance")
+        scale_and_quantise(val_banks[0], vsc_col, val_codes[0], val_scales[0], "val_bf0")
 
+        gather_vals(2, False, "guess_pool")
+        warm_exp = keep.tile([P, 1], F32, name="warm_exp")
+        nc.scalar.activation(warm_exp[:], log_chance[:, PACK - 1, 0:1], ACT.Exp)
         neg_s = keep.tile([P, I], F32, name="neg_s")
         neg_max = keep.tile([P, 1], F32, name="neg_max")
         nc.vector.tensor_scalar(neg_s[:], log_bank[:].rearrange("p j s -> p (j s)"), neg_lam[:], None, ALU.mult, ALU.min, accum_out=neg_max[:])
-        neg_sum = keep.tile([P, 1], F32, name="neg_sum")
-        nc.vector.tensor_reduce(neg_sum[:], neg_s[:], AXIS_X, ALU.add)
-        mean_less_max = keep.tile([P, 1], F32, name="mean_less_max")
-        nc.vector.tensor_scalar(mean_less_max[:], neg_sum[:], -1.0 / I, neg_max[:], ALU.mult, ALU.add)
+        log_sum = keep.tile([P, 1], F32, name="log_sum")
+        nc.vector.tensor_reduce(log_sum[:], log_sum_bank[:], AXIS_X, ALU.add)
+        mean_less_max = keep.tile([P, 1], F32, name="mean_less_max", tag="slot_c", align_bytes=64)
+        nc.vector.tensor_scalar(mean_less_max[:], log_sum[:], lam_share[:], neg_max[:], ALU.mult, ALU.add)
         probs = keep.tile([P, I], F32, name="probs")
         prob_sum = keep.tile([P, 1], F32, name="prob_sum")
         nc.scalar.activation(probs[:], neg_s[:], ACT.Exp, bias=neg_max[:], scale=-1.0, accum_out=prob_sum[:])
         odds = keep.tile([P, 1], F32, name="odds")
         nc.scalar.activation(odds[:], mean_less_max[:], ACT.Exp, bias=thresh_col[:], scale=eager_col[:])
 
-        scale_and_quantise(val_banks[0], vsc_col, val_codes[0], val_scales[0], "val_bf0")
-        gather_vals(2, False)
+        turn_vals(1, "bank_c")
         scale_and_quantise(val_banks[1], vsc_col, val_codes[1], val_scales[1], "val_bf1")
 
         denom = keep.tile([P, 1], F32, name="denom")
@@ -197,12 +223,14 @@ def tile_attend_answerodds_abstaining_centredvalues_kernel(
         weight_bank = psum.tile([P, PACK, Q], F32, name="weight_bank", tag="bank_a")
         for t in range(PACK):
             nc.tensor.transpose(weight_bank[:, t, :], weights[:, t, :], ident[:])
-        centre_vals(2)
-        gather_vals(3, False)
+        centre_vals(2, "log_sum", "mean2")
+        turn_vals(2, "log_bank")
+        gather_vals(3, False, "slot_d")
         weight_codes = keep.tile([P, Q], U32, name="weight_codes", align_bytes=64)
         weight_scales = keep.tile([P, Q], U8, name="weight_scales", align_bytes=64)
         scale_and_quantise(weight_bank, factor_col, weight_codes, weight_scales, "weight_bf")
-        centre_vals(3)
+        centre_vals(3, "sums3", "mean3")
+        turn_vals(3, "bank_f")
         scale_and_quantise(val_banks[2], vsc_col, val_codes[2], val_scales[2], "val_bf2")
 
         def product(bank_cols, b):
@@ -212,7 +240,7 @@ def tile_attend_answerodds_abstaining_centredvalues_kernel(
             )
 
         last = BLOCKS - 1
-        early_bank = psum.tile([P, last, P], F32, name="early_bank", tag="bank_b")
+        early_bank = psum.tile([P, last, P], F32, name="early_bank")
         for b in range(last):
             product(early_bank[:, b, :], b)
         early_out = keep.tile([P, last * P], F32, name="early_out")
@@ -220,7 +248,7 @@ def tile_attend_answerodds_abstaining_centredvalues_kernel(
         nc.sync.dma_start(out[:, 0 : last * P], early_out[:])
 
         scale_and_quantise(val_banks[last], vsc_col, val_codes[last], val_scales[last], "val_bf3")
-        last_bank = psum.tile([P, P], F32, name="last_bank", tag="bank_c")
+        last_bank = psum.tile([P, P], F32, name="last_bank")
         product(last_bank[:], last)
         last_out = keep.tile([P, P], F32, name="last_out")
         nc.scalar.copy(last_out[:], last_bank[:])

@@ -43,14 +43,16 @@ def tile_attend_answerodds_abstaining_centredvalues_kernel(
         val_pool = [keep.tile([P, T], F32, name=f"val_pool{b}", align_bytes=64) for b in range(BLOCKS)]
 
         nc.vector.memset(key_bytes[:].bitcast(I32), 0)
-        nc.vector.memset(thr_pool[0:ROW, :], 0.0)
-        nc.vector.memset(steep_pool[0:ROW, :], 0.0)
-        nc.vector.memset(guess_pool[0:ROW, :], 0.0)
+        ident = keep.tile([P, P], F32, name="ident")
+        nc.vector.memset(ident[:], 0.0)
+        nc.vector.memset(thr_pool[0:ROW, 0 : T - 1], 0.0)
+        nc.vector.memset(thr_pool[0:ROW, T - 1 : T], 0.0)
 
         zero_col = keep.tile([P, 1], F32, name="zero_col")
         nc.gpsimd.memset(zero_col[:], 0.0)
-        ident = keep.tile([P, P], F32, name="ident")
-        make_identity(nc, ident[:])
+        nc.gpsimd.memset(steep_pool[0:ROW, :], 0.0)
+        make_identity(nc, ident[:], nomemset=True)
+        nc.gpsimd.memset(guess_pool[0:ROW, :], 0.0)
 
         nc.sync.dma_start(offsets[:], offs)
         nc.scalar.dma_start(steep_pool[ROW:P, :], steep[0:1, :])
@@ -68,6 +70,7 @@ def tile_attend_answerodds_abstaining_centredvalues_kernel(
         thresh_col = keep.tile([P, 1], F32, name="thresh_col")
         factor_col = keep.tile([P, PACK], F32, name="factor_col")
         loads_after_block = {
+            1: [(vsc_col, vsc.rearrange("o (p t) -> (o p) t", t=PACK)), (lam_col, lam)],
             2: [(eager_col, eager), (thresh_col, thresh)],
             3: [(factor_col, slot_factor.rearrange("o (p t) -> (o p) t", t=PACK))],
         }
@@ -80,22 +83,22 @@ def tile_attend_answerodds_abstaining_centredvalues_kernel(
             for j in range(PACK):
                 nc.tensor.transpose(bank[:, j, :], row_tile[:, j * P : (j + 1) * P], ident[:])
 
-        thr_row = keep.tile([P, I], F32, name="thr_row")
-        nc.scalar.activation(thr_row[:], thr_pool[:].indirect(offsets[:]), ACT.Copy)
         steep_row = keep.tile([P, I], F32, name="steep_row")
         nc.scalar.activation(steep_row[:], steep_pool[:].indirect(offsets[:]), ACT.Copy)
-        thr_bank = psum.tile([P, PACK, P], F32, name="thr_bank", tag="bank_a")
-        turn_row(thr_row, thr_bank)
-        steep_bank = psum.tile([P, PACK, P], F32, name="steep_bank", tag="bank_b")
+        thr_row = keep.tile([P, I], F32, name="thr_row")
+        nc.scalar.activation(thr_row[:], thr_pool[:].indirect(offsets[:]), ACT.Copy)
+        steep_bank = psum.tile([P, PACK, P], F32, name="steep_bank", tag="bank_a")
         turn_row(steep_row, steep_bank)
-        neg_thr_col = keep.tile([P, PACK], F32, name="neg_thr_col")
-        nc.scalar.activation(neg_thr_col[:], thr_bank[:, :, ROW], ACT.Copy, scale=-1.0)
+        thr_bank = psum.tile([P, PACK, P], F32, name="thr_bank", tag="bank_b")
+        turn_row(thr_row, thr_bank)
         steep_col = keep.tile([P, PACK], F32, name="steep_col")
         nc.scalar.activation(steep_col[:], steep_bank[:, :, ROW], ACT.Copy)
-        shift_col = keep.tile([P, PACK], F32, name="shift_col")
-        nc.gpsimd.tensor_tensor(shift_col[:], neg_thr_col[:], steep_col[:], ALU.mult)
         guess_row = keep.tile([P, I], F32, name="guess_row")
         nc.scalar.activation(guess_row[:], guess_pool[:].indirect(offsets[:]), ACT.Copy)
+        neg_thr_col = keep.tile([P, PACK], F32, name="neg_thr_col", tag="guess_pool", align_bytes=64)
+        nc.scalar.activation(neg_thr_col[:], thr_bank[:, :, ROW], ACT.Copy, scale=-1.0)
+        shift_col = keep.tile([P, PACK], F32, name="shift_col")
+        nc.gpsimd.tensor_tensor(shift_col[:], neg_thr_col[:], steep_col[:], ALU.mult)
         guess_bank = psum.tile([P, PACK, P], F32, name="guess_bank", tag="bank_c")
         turn_row(guess_row, guess_bank)
         guess_col = keep.tile([P, PACK], F32, name="guess_col")
@@ -103,18 +106,15 @@ def tile_attend_answerodds_abstaining_centredvalues_kernel(
         rest_col = keep.tile([P, PACK], F32, name="rest_col")
         nc.gpsimd.tensor_scalar(rest_col[:], guess_col[:], -1.0, 1.0, ALU.mult, ALU.add)
 
-        nc.scalar.dma_start(vsc_col[:], vsc.rearrange("o (p t) -> (o p) t", t=PACK))
-        nc.scalar.dma_start(lam_col[:], lam)
-
         picked_bytes = keep.tile([P, I], U8, name="picked_bytes", align_bytes=64)
         nc.vector.tensor_copy(picked_bytes[:], key_bytes[:].indirect(offsets[:]))
         query_bf = keep.tile([P, Q, PACK], BF16, name="query_bf", align_bytes=64)
         nc.vector.tensor_copy(query_bf[:], query_raw[:].rearrange("p t q -> p q t"))
+        picked_words = keep.tile([P, I], U32, name="picked_words", tag="slot_k", align_bytes=64)
+        nc.vector.tensor_copy(picked_words[:], key_words[:].indirect(offsets[:]))
         query_codes = keep.tile([P, Q], U32, name="query_codes", align_bytes=64)
         query_scales = keep.tile([P, Q], U8, name="query_scales", align_bytes=64)
         nc.vector.quantize_mx(query_codes[:].bitcast(FP8X4), query_scales[:], query_bf[:].rearrange("p q t -> p (q t)"))
-        picked_words = keep.tile([P, I], U32, name="picked_words", tag="query_raw", align_bytes=64)
-        nc.vector.tensor_copy(picked_words[:], key_words[:].indirect(offsets[:]))
 
         score_bank = psum.tile([P, PACK, Q], F32, name="score_bank", tag="bank_b")
         for j in range(PACK):
@@ -127,8 +127,6 @@ def tile_attend_answerodds_abstaining_centredvalues_kernel(
         for j in range(PACK):
             nc.scalar.activation(sig[:, j, :], score_bank[:, j, :], ACT.Sigmoid, bias=shift_col[:, j : j + 1], scale=steep_col[:, j : j + 1])
 
-        warm_ln = keep.tile([P, 1], F32, name="warm_ln")
-        nc.scalar.activation(warm_ln[:], sig[:, PACK - 1, 0:1], ACT.Ln)
         neg_lam = keep.tile([P, 1], F32, name="neg_lam")
         nc.gpsimd.tensor_scalar(neg_lam[:], lam_col[:], -1.0, 0.0, ALU.mult, ALU.add)
 
@@ -151,6 +149,7 @@ def tile_attend_answerodds_abstaining_centredvalues_kernel(
         val_scales = [keep.tile([P, P], U8, name=f"val_scales{b}", align_bytes=64) for b in range(BLOCKS)]
         val_banks = {}
         neg_means = {}
+        sums = {}
 
         def gather_vals(b, on_vector, tag):
             picked_vals[b] = keep.tile([P, I], F32, name=f"picked_vals{b}", tag=tag, align_bytes=64)
@@ -160,14 +159,19 @@ def tile_attend_answerodds_abstaining_centredvalues_kernel(
             else:
                 nc.scalar.activation(picked_vals[b][:], window, ACT.Copy)
 
-        def centre_vals(b, sums_tag, mean_tag):
-            sums = keep.tile([P, H], F32, name=f"sums{b}", tag=sums_tag)
-            nc.vector.tensor_reduce(sums[:], picked_vals[b][:].rearrange("p (h s) -> p h s", s=STRETCH), AXIS_X, ALU.add)
-            neg_mean = keep.tile([P, H, PACK], F32, name=f"neg_mean{b}", tag=mean_tag)
+        def sum_vals(b, tag):
+            sums[b] = keep.tile([P, H], F32, name=f"sums{b}", tag=tag)
+            nc.vector.tensor_reduce(sums[b][:], picked_vals[b][:].rearrange("p (h s) -> p h s", s=STRETCH), AXIS_X, ALU.add)
+
+        def spread_mean(b, tag):
+            neg_means[b] = keep.tile([P, H, PACK], F32, name=f"neg_mean{b}", tag=tag)
             nc.vector.tensor_scalar(
-                neg_mean[:], sums[:].rearrange("p (h o) -> p h o", o=1).to_broadcast([P, H, PACK]), -1.0 / STRETCH, None, ALU.mult
+                neg_means[b][:], sums[b][:].rearrange("p (h o) -> p h o", o=1).to_broadcast([P, H, PACK]), -1.0 / STRETCH, None, ALU.mult
             )
-            neg_means[b] = neg_mean
+
+        def centre_vals(b, sums_tag, mean_tag):
+            sum_vals(b, sums_tag)
+            spread_mean(b, mean_tag)
 
         def turn_vals(b, bank_tag):
             neg_mean = neg_means[b]
@@ -180,8 +184,8 @@ def tile_attend_answerodds_abstaining_centredvalues_kernel(
                 )
             val_banks[b] = bank
 
-        def scale_and_quantise(bank, col, codes, scales, name):
-            staged = keep.tile([P, P, PACK], BF16, name=name, align_bytes=64)
+        def scale_and_quantise(bank, col, codes, scales, name, tag):
+            staged = keep.tile([P, P, PACK], BF16, name=name, tag=tag, align_bytes=64)
             nc.vector.tensor_tensor(
                 staged[:], bank[:].rearrange("p t x -> p x t"),
                 col[:].rearrange("p (o t) -> p o t", o=1).to_broadcast([P, P, PACK]), ALU.mult,
@@ -190,10 +194,10 @@ def tile_attend_answerodds_abstaining_centredvalues_kernel(
 
         gather_vals(0, True, "slot_a")
         centre_vals(0, "sums0", "mean0")
-        turn_vals(0, "bank_b")
+        turn_vals(0, "bank_c")
         gather_vals(1, True, "slot_b")
-        centre_vals(1, "sums1", "log_chance")
-        scale_and_quantise(val_banks[0], vsc_col, val_codes[0], val_scales[0], "val_bf0")
+        sum_vals(1, "sums1")
+        scale_and_quantise(val_banks[0], vsc_col, val_codes[0], val_scales[0], "val_bf0", "val_bf0")
 
         gather_vals(2, False, "guess_pool")
         warm_exp = keep.tile([P, 1], F32, name="warm_exp")
@@ -201,37 +205,38 @@ def tile_attend_answerodds_abstaining_centredvalues_kernel(
         neg_s = keep.tile([P, I], F32, name="neg_s")
         neg_max = keep.tile([P, 1], F32, name="neg_max")
         nc.vector.tensor_scalar(neg_s[:], log_bank[:].rearrange("p j s -> p (j s)"), neg_lam[:], None, ALU.mult, ALU.min, accum_out=neg_max[:])
-        log_sum = keep.tile([P, 1], F32, name="log_sum")
-        nc.vector.tensor_reduce(log_sum[:], log_sum_bank[:], AXIS_X, ALU.add)
-        mean_less_max = keep.tile([P, 1], F32, name="mean_less_max", tag="slot_c", align_bytes=64)
-        nc.vector.tensor_scalar(mean_less_max[:], log_sum[:], lam_share[:], neg_max[:], ALU.mult, ALU.add)
+        spread_mean(1, "log_chance")
+        turn_vals(1, "bank_b")
+        mean_less_max = keep.tile([P, 1], F32, name="mean_less_max")
+        shares = keep.tile([P, P], F32, name="shares")
+        nc.vector.tensor_scalar(shares[:], log_sum_bank[:], lam_share[:], neg_max[:], ALU.mult, ALU.add, accum_out=mean_less_max[:])
+        odds = keep.tile([P, 1], F32, name="odds")
+        nc.scalar.activation(odds[:], mean_less_max[:], ACT.Exp, bias=thresh_col[:], scale=eager_col[:])
         probs = keep.tile([P, I], F32, name="probs")
         prob_sum = keep.tile([P, 1], F32, name="prob_sum")
         nc.scalar.activation(probs[:], neg_s[:], ACT.Exp, bias=neg_max[:], scale=-1.0, accum_out=prob_sum[:])
-        odds = keep.tile([P, 1], F32, name="odds")
-        nc.scalar.activation(odds[:], mean_less_max[:], ACT.Exp, bias=thresh_col[:], scale=eager_col[:])
-
-        turn_vals(1, "bank_c")
-        scale_and_quantise(val_banks[1], vsc_col, val_codes[1], val_scales[1], "val_bf1")
-
-        denom = keep.tile([P, 1], F32, name="denom")
-        nc.vector.tensor_scalar(denom[:], odds[:], 1.0, prob_sum[:], ALU.add, ALU.mult)
-        gain = keep.tile([P, 1], F32, name="gain")
-        nc.vector.reciprocal(gain[:], denom[:])
+        gather_vals(3, False, "slot_d")
+        centre_vals(2, "neg_lam", "mean2")
+        turn_vals(2, "log_bank")
+        odds_and_one = keep.tile([P, 1], F32, name="odds_and_one")
+        nc.gpsimd.tensor_scalar(odds_and_one[:], odds[:], 1.0, 1.0, ALU.mult, ALU.add)
+        gate = keep.tile([P, 1], F32, name="gate")
+        nc.vector.reciprocal(gate[:], odds_and_one[:])
+        inv_sum = keep.tile([P, 1], F32, name="inv_sum")
+        nc.vector.reciprocal(inv_sum[:], prob_sum[:])
         weights = keep.tile([P, PACK, P], F32, name="weights")
-        nc.vector.tensor_scalar(weights[:], probs[:].rearrange("q (p t) -> q t p", t=PACK), gain[:], None, ALU.mult)
+        nc.vector.tensor_scalar(weights[:], probs[:].rearrange("q (p t) -> q t p", t=PACK), inv_sum[:], gate[:], ALU.mult, ALU.mult)
         weight_bank = psum.tile([P, PACK, Q], F32, name="weight_bank", tag="bank_a")
         for t in range(PACK):
             nc.tensor.transpose(weight_bank[:, t, :], weights[:, t, :], ident[:])
-        centre_vals(2, "log_sum", "mean2")
-        turn_vals(2, "log_bank")
-        gather_vals(3, False, "slot_d")
-        weight_codes = keep.tile([P, Q], U32, name="weight_codes", align_bytes=64)
-        weight_scales = keep.tile([P, Q], U8, name="weight_scales", align_bytes=64)
-        scale_and_quantise(weight_bank, factor_col, weight_codes, weight_scales, "weight_bf")
+        scale_and_quantise(val_banks[1], vsc_col, val_codes[1], val_scales[1], "val_bf1", "val_bf1")
         centre_vals(3, "sums3", "mean3")
         turn_vals(3, "bank_f")
-        scale_and_quantise(val_banks[2], vsc_col, val_codes[2], val_scales[2], "val_bf2")
+        weight_codes = keep.tile([P, Q], U32, name="weight_codes", align_bytes=64)
+        weight_scales = keep.tile([P, Q], U8, name="weight_scales", align_bytes=64)
+        scale_and_quantise(val_banks[2], vsc_col, val_codes[2], val_scales[2], "val_bf2", "val_bf2")
+        scale_and_quantise(weight_bank, factor_col, weight_codes, weight_scales, "weight_bf", "weight_bf")
+        scale_and_quantise(val_banks[3], vsc_col, val_codes[3], val_scales[3], "val_bf3", "val_bf3")
 
         def product(bank_cols, b):
             nc.tensor.matmul_mx(
@@ -247,7 +252,6 @@ def tile_attend_answerodds_abstaining_centredvalues_kernel(
         nc.scalar.copy(early_out[:], early_bank[:].rearrange("p b x -> p (b x)"))
         nc.sync.dma_start(out[:, 0 : last * P], early_out[:])
 
-        scale_and_quantise(val_banks[last], vsc_col, val_codes[last], val_scales[last], "val_bf3")
         last_bank = psum.tile([P, P], F32, name="last_bank")
         product(last_bank[:], last)
         last_out = keep.tile([P, P], F32, name="last_out")

from contextlib import ExitStack

import concourse.mybir as mybir
from concourse.masks import make_identity

D, T, I, Q, E, H = 512, 2048, 512, 128, 512, 32
FLOPS = 2 * Q * I * D + 2 * Q * I * E
BYTES = 4 * D * Q + D * T + 16 * T + 3 * 4 * T + 3 * 4 * Q + 2 * 4 * I + 4 * E * T + 2 * I + 4 * Q * E

F32 = mybir.dt.float32
BF16 = mybir.dt.bfloat16
I32 = mybir.dt.int32
U32 = mybir.dt.uint32
U16 = mybir.dt.uint16
U8 = mybir.dt.uint8
FP8X4 = mybir.dt.float8_e4m3fn_x4
ALU = mybir.AluOpType
ACT = mybir.ActivationFunctionType
AXIS_X = mybir.AxisListType.X

P = 128
PACK = 4
STRETCH = I // H
BLOCKS = E // P
ROW = P - 1


def tile_attend_answerodds_abstaining_centredvalues_kernel(
    tc, query, keys_words, keys_scales, guess, steep, thr, lam, eager, thresh, slot_factor, vals, vsc, offs, out
):
    nc = tc.nc
    with ExitStack() as ctx:
        keep = ctx.enter_context(tc.tile_pool(name="keep", bufs=1))
        psum = ctx.enter_context(tc.psum_pool(name="psum", bufs=1))

        offsets = keep.tile([P, I // 16], U16, name="offsets")
        key_words = keep.tile([P, T], U32, name="key_words")
        key_bytes = keep.tile([P, T], U8, name="key_bytes", tag="slot_k", align_bytes=64)
        thr_pool = keep.tile([P, T], F32, name="thr_pool")
        steep_pool = keep.tile([P, T], F32, name="steep_pool")
        guess_pool = keep.tile([P, T], F32, name="guess_pool", align_bytes=64)
        query_raw = keep.tile([P, PACK, Q], F32, name="query_raw", align_bytes=64)
        val_pool = [keep.tile([P, T], F32, name=f"val_pool{b}", align_bytes=64) for b in range(BLOCKS)]

        nc.vector.memset(key_bytes[:].bitcast(I32), 0)
        ident = keep.tile([P, P], F32, name="ident")
        nc.vector.memset(ident[:], 0.0)
        nc.vector.memset(thr_pool[0:ROW, 0 : T - 1], 0.0)
        nc.vector.memset(thr_pool[0:ROW, T - 1 : T], 0.0)

        zero_col = keep.tile([P, 1], F32, name="zero_col")
        nc.gpsimd.memset(zero_col[:], 0.0)
        nc.gpsimd.memset(steep_pool[0:ROW, :], 0.0)
        make_identity(nc, ident[:], nomemset=True)
        nc.gpsimd.memset(guess_pool[0:ROW, :], 0.0)

        nc.sync.dma_start(offsets[:], offs)
        nc.scalar.dma_start(steep_pool[ROW:P, :], steep[0:1, :])
        nc.scalar.dma_start(key_words[:].bitcast(I32), keys_words[0].rearrange("p n t -> p (n t)").bitcast(I32))
        warm = keep.tile([P, 1], F32, name="warm")
        nc.scalar.activation(warm[:], zero_col[:], ACT.Sigmoid)
        nc.scalar.dma_start(guess_pool[ROW:P, :], guess[0:1, :])
        nc.sync.dma_start(thr_pool[ROW:P, :], thr[0:1, :])
        for g in range(4):
            nc.sync.dma_start(key_bytes[32 * g : 32 * g + 4, :].bitcast(I32), keys_scales[0, 4 * g : 4 * g + 4, :].bitcast(I32))
        nc.sync.dma_start(query_raw[:], query.rearrange("(p t) q -> p t q", t=PACK))
        vsc_col = keep.tile([P, PACK], F32, name="vsc_col")
        lam_col = keep.tile([P, 1], F32, name="lam_col")
        eager_col = keep.tile([P, 1], F32, name="eager_col")
        thresh_col = keep.tile([P, 1], F32, name="thresh_col")
        factor_col = keep.tile([P, PACK], F32, name="factor_col")
        loads_after_block = {
            1: [(vsc_col, vsc.rearrange("o (p t) -> (o p) t", t=PACK)), (lam_col, lam)],
            2: [(eager_col, eager), (thresh_col, thresh)],
            3: [(factor_col, slot_factor.rearrange("o (p t) -> (o p) t", t=PACK))],
        }
        for b in range(BLOCKS):
            nc.sync.dma_start(val_pool[b][:], vals[b * P : (b + 1) * P, :])
            for column, source in loads_after_block.get(b, []):
                nc.sync.dma_start(column[:], source)

        def turn_row(row_tile, bank):
            for j in range(PACK):
                nc.tensor.transpose(bank[:, j, :], row_tile[:, j * P : (j + 1) * P], ident[:])

        steep_row = keep.tile([P, I], F32, name="steep_row")
        nc.scalar.activation(steep_row[:], steep_pool[:].indirect(offsets[:]), ACT.Copy)
        thr_row = keep.tile([P, I], F32, name="thr_row")
        nc.scalar.activation(thr_row[:], thr_pool[:].indirect(offsets[:]), ACT.Copy)
        steep_bank = psum.tile([P, PACK, P], F32, name="steep_bank", tag="bank_a")
        turn_row(steep_row, steep_bank)
        thr_bank = psum.tile([P, PACK, P], F32, name="thr_bank", tag="bank_b")
        turn_row(thr_row, thr_bank)
        steep_col = keep.tile([P, PACK], F32, name="steep_col")
        nc.scalar.activation(steep_col[:], steep_bank[:, :, ROW], ACT.Copy)
        guess_row = keep.tile([P, I], F32, name="guess_row")
        nc.scalar.activation(guess_row[:], guess_pool[:].indirect(offsets[:]), ACT.Copy)
        neg_thr_col = keep.tile([P, PACK], F32, name="neg_thr_col", tag="guess_pool", align_bytes=64)
        nc.scalar.activation(neg_thr_col[:], thr_bank[:, :, ROW], ACT.Copy, scale=-1.0)
        shift_col = keep.tile([P, PACK], F32, name="shift_col")
        nc.gpsimd.tensor_tensor(shift_col[:], neg_thr_col[:], steep_col[:], ALU.mult)
        guess_bank = psum.tile([P, PACK, P], F32, name="guess_bank", tag="bank_c")
        turn_row(guess_row, guess_bank)
        guess_col = keep.tile([P, PACK], F32, name="guess_col")
        nc.scalar.activation(guess_col[:], guess_bank[:, :, ROW], ACT.Copy)
        rest_col = keep.tile([P, PACK], F32, name="rest_col")
        nc.gpsimd.tensor_scalar(rest_col[:], guess_col[:], -1.0, 1.0, ALU.mult, ALU.add)

        picked_bytes = keep.tile([P, I], U8, name="picked_bytes", align_bytes=64)
        nc.vector.tensor_copy(picked_bytes[:], key_bytes[:].indirect(offsets[:]))
        query_bf = keep.tile([P, Q, PACK], BF16, name="query_bf", align_bytes=64)
        nc.vector.tensor_copy(query_bf[:], query_raw[:].rearrange("p t q -> p q t"))
        picked_words = keep.tile([P, I], U32, name="picked_words", tag="slot_k", align_bytes=64)
        nc.vector.tensor_copy(picked_words[:], key_words[:].indirect(offsets[:]))
        query_codes = keep.tile([P, Q], U32, name="query_codes", align_bytes=64)
        query_scales = keep.tile([P, Q], U8, name="query_scales", align_bytes=64)
        nc.vector.quantize_mx(query_codes[:].bitcast(FP8X4), query_scales[:], query_bf[:].rearrange("p q t -> p (q t)"))

        score_bank = psum.tile([P, PACK, Q], F32, name="score_bank", tag="bank_b")
        for j in range(PACK):
            cols = slice(j * P, (j + 1) * P)
            nc.tensor.matmul_mx(
                score_bank[:, j, :], lhsT=picked_words[:, cols].bitcast(FP8X4), lhsT_scale=picked_bytes[:, cols],
                rhs=query_codes[:].bitcast(FP8X4), rhs_scale=query_scales[:], start=True, stop=True,
            )
        sig = keep.tile([P, PACK, Q], F32, name="sig", tag="guess_pool", align_bytes=64)
        for j in range(PACK):
            nc.scalar.activation(sig[:, j, :], score_bank[:, j, :], ACT.Sigmoid, bias=shift_col[:, j : j + 1], scale=steep_col[:, j : j + 1])

        neg_lam = keep.tile([P, 1], F32, name="neg_lam")
        nc.gpsimd.tensor_scalar(neg_lam[:], lam_col[:], -1.0, 0.0, ALU.mult, ALU.add)

        lam_share = keep.tile([P, 1], F32, name="lam_share")
        nc.gpsimd.tensor_scalar(lam_share[:], lam_col[:], 1.0 / I, 0.0, ALU.mult, ALU.add)

        log_chance = keep.tile([P, PACK, Q], F32, name="log_chance")
        for j in range(PACK):
            nc.scalar.activation(log_chance[:, j, :], sig[:, j, :], ACT.Ln, bias=guess_col[:, j : j + 1], scale=rest_col[:, j : j + 1])
        log_bank = psum.tile([P, PACK, P], F32, name="log_bank")
        for j in range(PACK):
            nc.tensor.transpose(log_bank[:, j, :], log_chance[:, j, :], ident[:])

        log_sum_bank = psum.tile([P, P], F32, name="log_sum_bank")
        for j in range(PACK):
            nc.tensor.matmul(log_sum_bank[:], log_chance[:, j, :], ident[:], start=(j == 0), stop=(j == PACK - 1), is_transpose=True)

        picked_vals = {}
        val_codes = [keep.tile([P, P], U32, name=f"val_codes{b}", align_bytes=64) for b in range(BLOCKS)]
        val_scales = [keep.tile([P, P], U8, name=f"val_scales{b}", align_bytes=64) for b in range(BLOCKS)]
        val_banks = {}
        neg_means = {}
        sums = {}

        def gather_vals(b, on_vector, tag):
            picked_vals[b] = keep.tile([P, I], F32, name=f"picked_vals{b}", tag=tag, align_bytes=64)
            window = val_pool[b][:].indirect(offsets[:])
            if on_vector:
                nc.vector.tensor_copy(picked_vals[b][:], window)
            else:
                nc.scalar.activation(picked_vals[b][:], window, ACT.Copy)

        def sum_vals(b, tag):
            sums[b] = keep.tile([P, H], F32, name=f"sums{b}", tag=tag)
            nc.vector.tensor_reduce(sums[b][:], picked_vals[b][:].rearrange("p (h s) -> p h s", s=STRETCH), AXIS_X, ALU.add)

        def spread_mean(b, tag):
            neg_means[b] = keep.tile([P, H, PACK], F32, name=f"neg_mean{b}", tag=tag)
            nc.vector.tensor_scalar(
                neg_means[b][:], sums[b][:].rearrange("p (h o) -> p h o", o=1).to_broadcast([P, H, PACK]), -1.0 / STRETCH, None, ALU.mult
            )

        def centre_vals(b, sums_tag, mean_tag):
            sum_vals(b, sums_tag)
            spread_mean(b, mean_tag)

        def turn_vals(b, bank_tag):
            neg_mean = neg_means[b]
            bank = psum.tile([P, PACK, P], F32, name=f"val_bank{b}", tag=bank_tag)
            for t in range(PACK):
                nc.tensor.matmul(bank[:, t, :], picked_vals[b][:, t : I : PACK], ident[:], start=(t == 0), stop=False, is_transpose=True)
            for t in range(PACK):
                nc.tensor.matmul(
                    bank[:, t, :], neg_mean[:].rearrange("p h r -> p (h r)"), ident[:], start=False, stop=(t == PACK - 1), is_transpose=True
                )
            val_banks[b] = bank

        def scale_and_quantise(bank, col, codes, scales, name, tag):
            staged = keep.tile([P, P, PACK], BF16, name=name, tag=tag, align_bytes=64)
            nc.vector.tensor_tensor(
                staged[:], bank[:].rearrange("p t x -> p x t"),
                col[:].rearrange("p (o t) -> p o t", o=1).to_broadcast([P, P, PACK]), ALU.mult,
            )
            nc.vector.quantize_mx(codes[:].bitcast(FP8X4), scales[:], staged[:].rearrange("p x t -> p (x t)"))

        gather_vals(0, True, "slot_a")
        centre_vals(0, "sums0", "mean0")
        turn_vals(0, "bank_c")
        gather_vals(1, True, "slot_b")
        sum_vals(1, "sums1")
        scale_and_quantise(val_banks[0], vsc_col, val_codes[0], val_scales[0], "val_bf0", "val_bf0")

        gather_vals(2, False, "guess_pool")
        warm_exp = keep.tile([P, 1], F32, name="warm_exp")
        nc.scalar.activation(warm_exp[:], log_chance[:, PACK - 1, 0:1], ACT.Exp)
        neg_s = keep.tile([P, I], F32, name="neg_s")
        neg_max = keep.tile([P, 1], F32, name="neg_max")
        nc.vector.tensor_scalar(neg_s[:], log_bank[:].rearrange("p j s -> p (j s)"), neg_lam[:], None, ALU.mult, ALU.min, accum_out=neg_max[:])
        spread_mean(1, "log_chance")
        turn_vals(1, "bank_b")
        mean_less_max = keep.tile([P, 1], F32, name="mean_less_max")
        shares = keep.tile([P, P], F32, name="shares")
        nc.vector.tensor_scalar(shares[:], log_sum_bank[:], lam_share[:], neg_max[:], ALU.mult, ALU.add, accum_out=mean_less_max[:])
        odds = keep.tile([P, 1], F32, name="odds")
        nc.scalar.activation(odds[:], mean_less_max[:], ACT.Exp, bias=thresh_col[:], scale=eager_col[:])
        probs = keep.tile([P, I], F32, name="probs")
        prob_sum = keep.tile([P, 1], F32, name="prob_sum")
        nc.scalar.activation(probs[:], neg_s[:], ACT.Exp, bias=neg_max[:], scale=-1.0, accum_out=prob_sum[:])
        gather_vals(3, False, "slot_d")
        centre_vals(2, "neg_lam", "mean2")
        turn_vals(2, "log_bank")
        odds_and_one = keep.tile([P, 1], F32, name="odds_and_one")
        nc.gpsimd.tensor_scalar(odds_and_one[:], odds[:], 1.0, 1.0, ALU.mult, ALU.add)
        gate = keep.tile([P, 1], F32, name="gate")
        nc.vector.reciprocal(gate[:], odds_and_one[:])
        inv_sum = keep.tile([P, 1], F32, name="inv_sum")
        nc.vector.reciprocal(inv_sum[:], prob_sum[:])
        weights = keep.tile([P, PACK, P], F32, name="weights")
        nc.vector.tensor_scalar(weights[:], probs[:].rearrange("q (p t) -> q t p", t=PACK), inv_sum[:], gate[:], ALU.mult, ALU.mult)
        weight_bank = psum.tile([P, PACK, Q], F32, name="weight_bank", tag="bank_a")
        for t in range(PACK):
            nc.tensor.transpose(weight_bank[:, t, :], weights[:, t, :], ident[:])
        scale_and_quantise(val_banks[1], vsc_col, val_codes[1], val_scales[1], "val_bf1", "val_bf1")
        centre_vals(3, "sums3", "mean3")
        turn_vals(3, "bank_f")
        weight_codes = keep.tile([P, Q], U32, name="weight_codes", align_bytes=64)
        weight_scales = keep.tile([P, Q], U8, name="weight_scales", align_bytes=64)
        scale_and_quantise(val_banks[2], vsc_col, val_codes[2], val_scales[2], "val_bf2", "val_bf2")
        scale_and_quantise(weight_bank, factor_col, weight_codes, weight_scales, "weight_bf", "weight_bf")
        scale_and_quantise(val_banks[3], vsc_col, val_codes[3], val_scales[3], "val_bf3", "val_bf3")

        def product(bank_cols, b):
            nc.tensor.matmul_mx(
                bank_cols, lhsT=weight_codes[:].bitcast(FP8X4), lhsT_scale=weight_scales[:],
                rhs=val_codes[b][:].bitcast(FP8X4), rhs_scale=val_scales[b][:], start=True, stop=True,
            )

        last = BLOCKS - 1
        early_bank = psum.tile([P, last, P], F32, name="early_bank")
        for b in range(last):
            product(early_bank[:, b, :], b)
        early_out = keep.tile([P, last * P], F32, name="early_out")
        nc.scalar.copy(early_out[:], early_bank[:].rearrange("p b x -> p (b x)"))
        nc.sync.dma_start(out[:, 0 : last * P], early_out[:])

        last_bank = psum.tile([P, P], F32, name="last_bank")
        product(last_bank[:], last)
        last_out = keep.tile([P, P], F32, name="last_out")
        nc.scalar.copy(last_out[:], last_bank[:])
        nc.sync.dma_start(out[:, last * P : E], last_out[:])
